import numpy as np
import ml_dtypes


def mxq(x, axis, fmt="e4m3"):
    dtype, down = {"e4m3": (ml_dtypes.float8_e4m3fn, 7), "e5m2": (ml_dtypes.float8_e5m2, 14)}[fmt]
    v = np.moveaxis(np.asarray(x, np.float32).astype(ml_dtypes.bfloat16).astype(np.float64), axis, -1)
    blocks = v.reshape(v.shape[:-1] + (-1, 32))
    amax = np.abs(blocks).max(-1, keepdims=True)
    byte = np.maximum(np.where(amax > 0, np.frexp(amax)[1] - 1 + 127, 0) - down, 1)
    scale = np.exp2(byte - 127.0)
    codes = (blocks / scale).astype(np.float32).astype(dtype).astype(np.float64)
    return np.moveaxis((codes * scale).reshape(v.shape), -1, axis)


WIDE = False


def mx_kscale(k):
    if not WIDE:
        return np.ones(k)
    levels = np.array([10, -10, 5, -5, 0])
    if k % 512:
        return np.exp2(np.random.permutation(np.resize(levels, k // 32))).repeat(32)
    a = np.empty((k // 512, 16))
    for p in range(k // 512):
        a[p, :8] = np.random.permutation(np.resize(levels, 8))
        for g in range(8):
            far = levels[np.abs(levels - a[p, g]) >= 10]
            a[p, g + 8] = far[np.random.randint(len(far))]
    return np.exp2(a.ravel()).repeat(32)


def f64(x):
    return np.asarray(x).astype(np.float64)


def striped(idx):
    return np.tile(np.asarray(idx).reshape(-1, 16).T, (8, 1)).astype(np.uint16)


def unstriped(offs):
    return offs[:16].T.reshape(-1).astype(np.int64)


E2M1 = np.array([0.0, 0.5, 1.0, 1.5, 2.0, 3.0, 4.0, 6.0, -0.0, -0.5, -1.0, -1.5, -2.0, -3.0, -4.0, -6.0])


def pack_weight(w, fmt):
    k, n = w.shape
    w = f64(np.asarray(w, np.float32).astype(ml_dtypes.bfloat16)).reshape(k // 32, 32, n)
    amax = np.abs(w).max(1)
    if fmt == "e4m3":
        byte = np.frexp(amax)[1] - 1 + 127 - 7
    else:
        mant, ex = np.frexp(amax / 6.0)
        byte = np.where(mant > 0.5, ex, ex - 1) + 127
    byte = np.clip(np.where(amax > 0, byte, 1), 1, 254)
    scaled = (w * np.exp2(127.0 - byte)[:, None, :]).reshape(k, n).astype(np.float32)
    by_word = np.ascontiguousarray(scaled.reshape(k // 512, 128, 4, n).transpose(0, 1, 3, 2))
    if fmt == "e4m3":
        words = by_word.astype(ml_dtypes.float8_e4m3fn).view(np.uint8)
    else:
        c = by_word.astype(ml_dtypes.float4_e2m1fn).view(np.uint8) & 0xF
        words = (c[..., 0::2] | (c[..., 1::2] << 4)).reshape(k // 512, 128, 2 * n)
    return np.ascontiguousarray(words), np.ascontiguousarray(byte.astype(np.uint8).reshape(k // 512, 16, n))


def unpack_weight(words, scales, fmt):
    g, _, n = scales.shape
    words = np.ascontiguousarray(words).reshape(g, 128, n, -1)
    if fmt == "e4m3":
        vals = words.view(ml_dtypes.float8_e4m3fn).astype(np.float64)
    else:
        nib = np.empty((g, 128, n, 4), np.uint8)
        nib[..., 0::2] = words & 0xF
        nib[..., 1::2] = words >> 4
        vals = E2M1[nib]
    vals = vals * np.repeat(np.exp2(scales.astype(np.float64) - 127.0), 8, axis=1)[..., None]
    return vals.transpose(0, 1, 3, 2).reshape(g * 512, n)


def softplus(v):
    return np.log(1.0 + np.exp(v))


def sigmoid(v):
    return 1.0 / (1.0 + np.exp(-v))


D, E, T, I, Q = 512, 512, 2048, 512, 128


def setup_inputs():
    n = np.random.standard_normal
    idx = np.random.permutation(T)[:I]
    fd = mx_kscale(D)
    fi = mx_kscale(I)
    ti = np.ones(T)
    ti[idx] = fi
    keysp = pack_weight(n((D, T)) / fd[:, None], "e2m1")
    return {
        "query": (n((D, Q)) * 0.6 / np.sqrt(D) * fd[:, None]).astype(np.float32),
        "query2": (n((D, Q)) * 1.0 / np.sqrt(D) * fd[:, None]).astype(np.float32),
        "keys_words": keysp[0],
        "keys_scales": keysp[1],
        "strict": (np.random.uniform(0.4, 1.2, (Q, 1))).astype(np.float32),
        "dquery2": (n((D, Q)) * 0.6 / np.sqrt(D) * fd[:, None]).astype(np.float32),
        "os": (np.random.uniform(4.0, 16.0, (1, I)) * fi).astype(np.float32),
        "vals": (n((E, T)) / ti).astype(np.float32),
        "offs": striped(idx),
    }


def reference(query, query2, keys_words, keys_scales, strict, dquery2, os, vals, offs):
    idx = unstriped(offs)
    keysu = unpack_weight(keys_words, keys_scales, "e2m1")
    queryq = mxq(f64(query), 0, "e4m3")
    keysidxg = keysu[:, idx]
    a = queryq.T @ keysidxg
    query2q = mxq(f64(query2), 0, "e4m3")
    b = query2q.T @ keysidxg
    dquery2q = mxq(f64(dquery2), 0, "e4m3")
    tb = dquery2q.T @ keysidxg
    s = a - softplus(b) * f64(strict)
    p = np.exp(s - np.max(s, axis=1, keepdims=True))
    z = np.sum(p, axis=1, keepdims=True)
    ts = tb * sigmoid(b) * f64(strict) * (-1.0)
    tp = ts * p
    tz = np.sum(tp, axis=1, keepdims=True)
    tw = (tp - tz * p / z) / z
    wo1 = tw * f64(os)
    wt1 = wo1.T
    vt1 = f64(vals)[:, idx].T
    wt1q = mxq(wt1, 0, "e4m3")
    vt1q = mxq(vt1, 0, "e4m3")
    o = wt1q.T @ vt1q
    return o

@@ -1,0 +1,222 @@
+from contextlib import ExitStack
+
+import concourse.mybir as mybir
+from concourse.masks import make_identity
+
+F32 = mybir.dt.float32
+BF16 = mybir.dt.bfloat16
+I32 = mybir.dt.int32
+U32 = mybir.dt.uint32
+U16 = mybir.dt.uint16
+U8 = mybir.dt.uint8
+FP8X4 = mybir.dt.float8_e4m3fn_x4
+FP4X4 = mybir.dt.float4_e2m1fn_x4
+ALU = mybir.AluOpType
+ACT = mybir.ActivationFunctionType
+AX = mybir.AxisListType
+
+P = 128
+PACK = 4
+D, E, T, SLOTS, Q = 512, 512, 2048, 512, 128
+HALF = SLOTS // 2
+FLOPS = 2 * Q * SLOTS * (3 * D + E)
+
+
+def tile_attend_ttheldback_kernel(tc, query, query2, keys_words, keys_scales, strict, dquery2, slot_factor, vals, offs, out):
+    nc = tc.nc
+    with ExitStack() as ctx:
+        held = ctx.enter_context(tc.tile_pool(name="held", bufs=1))
+        psum = ctx.enter_context(tc.psum_pool(name="psum", bufs=1))
+
+        key_scale_pool = held.tile([P, T], U8, name="key_scale_pool", align_bytes=64)
+        nc.vector.memset(key_scale_pool[:].bitcast(I32), 0)
+        offsets = held.tile([P, SLOTS // 16], U16, name="offsets")
+        nc.sync.dma_start(offsets[:], offs)
+        for quad in range(4):
+            nc.scalar.dma_start(
+                key_scale_pool[32 * quad : 32 * quad + 4, :].bitcast(I32),
+                keys_scales[0, 4 * quad : 4 * quad + 4, :].bitcast(I32),
+            )
+        key_word_pool = held.tile([P, T], U16, name="key_word_pool", align_bytes=64)
+        nc.sync.dma_start(key_word_pool[:].bitcast(I32), keys_words[0].bitcast(I32))
+        raw = []
+        for name, source in (("b", query2), ("tb", dquery2), ("a", query)):
+            tile = held.tile([P, PACK, Q], F32, name="raw_" + name)
+            nc.sync.dma_start(tile[:], source.rearrange("(p t) q -> p t q", t=PACK))
+            raw.append(tile)
+        strict_col = held.tile([P, 1], F32, name="strict_col")
+        nc.gpsimd.dma_start(strict_col[:], strict)
+        os_cols = held.tile([P, PACK], F32, name="os_cols")
+        nc.gpsimd.dma_start(os_cols[:], slot_factor.rearrange("o (p t) -> (o p) t", t=PACK))
+        val_pool = []
+        for c in range(E // P):
+            tile = held.tile([P, T], F32, name="val_pool%d" % c)
+            nc.sync.dma_start(tile[:], vals[c * P : (c + 1) * P, :])
+            val_pool.append(tile)
+        ident = held.tile([P, P], F32, name="ident")
+        make_identity(nc, ident[:])
+
+        q_bf = held.tile([P, 3 * Q * PACK], BF16, name="q_bf", align_bytes=64)
+        q_codes = held.tile([P, 3 * Q], U32, name="q_codes", align_bytes=64)
+        q_scales = held.tile([P, 3 * Q], U8, name="q_scales", align_bytes=64)
+
+        def round_query(j):
+            nc.scalar.activation(
+                q_bf[:, j * Q * PACK : (j + 1) * Q * PACK].rearrange("p (q t) -> p q t", t=PACK),
+                raw[j][:].rearrange("p t q -> p q t"),
+                ACT.Copy,
+            )
+
+        def quantize_queries(j0, j1):
+            nc.vector.quantize_mx(
+                out=q_codes[:, j0 * Q : j1 * Q].bitcast(FP8X4),
+                scales=q_scales[:, j0 * Q : j1 * Q],
+                in_=q_bf[:, j0 * Q * PACK : j1 * Q * PACK],
+            )
+
+        key_words = held.tile([P, SLOTS], U16, name="key_words", align_bytes=64)
+        key_scales = held.tile([P, SLOTS], U8, name="key_scales", align_bytes=64)
+
+        def gather_keys(h):
+            cols = slice(h * HALF, (h + 1) * HALF)
+            part = offsets[:, h * HALF // 16 : (h + 1) * HALF // 16]
+            nc.vector.tensor_copy(key_words[:, cols], key_word_pool[:].indirect(part))
+            nc.vector.tensor_copy(key_scales[:, cols], key_scale_pool[:].indirect(part))
+
+        def scores(bank, j, cols):
+            nc.tensor.matmul_mx(
+                out=bank,
+                lhsT=q_codes[:, j * Q : (j + 1) * Q].bitcast(FP8X4),
+                lhsT_scale=q_scales[:, j * Q : (j + 1) * Q],
+                rhs=key_words[:, cols].bitcast(FP4X4),
+                rhs_scale=key_scales[:, cols],
+                start=True,
+                stop=True,
+            )
+
+        def dealt(bank):
+            return bank.rearrange("p (s r) -> p r s", r=PACK)
+
+        def half_of(tile, h):
+            return tile[:, :, h * (P // 2) : (h + 1) * (P // 2)]
+
+        round_query(0)
+        gather_keys(0)
+        quantize_queries(0, 1)
+        gather_keys(1)
+        round_query(1)
+        round_query(2)
+        b_banks = [psum.tile([P, HALF], F32, name="half_bank%d" % h) for h in range(2)]
+        th = held.tile([P, PACK, P], F32, name="th")
+        th_abs = held.tile([P, PACK, P], F32, name="th_abs")
+        for h in range(2):
+            scores(b_banks[h][:], 0, slice(h * HALF, (h + 1) * HALF))
+            nc.scalar.activation(half_of(th, h), dealt(b_banks[h][:]), ACT.Tanh, scale=0.5)
+            nc.scalar.activation(half_of(th_abs, h), half_of(th, h), ACT.Abs)
+        quantize_queries(1, 3)
+        tb_bank = psum.tile([P, SLOTS], F32, name="tb_bank")
+        a_bank = psum.tile([P, SLOTS], F32, name="a_bank")
+        scores(tb_bank[:], 1, slice(0, SLOTS))
+        scores(a_bank[:], 2, slice(0, SLOTS))
+
+        v_codes = held.tile([P, E], U32, name="v_codes", align_bytes=64)
+        v_scales = held.tile([P, E], U8, name="v_scales", align_bytes=64)
+
+        def values(c, gather_on_vector, tag):
+            picked = held.tile([P, SLOTS], BF16, name="picked%d" % c, tag=tag, align_bytes=64)
+            if gather_on_vector:
+                nc.vector.tensor_copy(picked[:], val_pool[c][:].indirect(offsets[:]))
+            else:
+                nc.scalar.activation(picked[:], val_pool[c][:].indirect(offsets[:]), ACT.Copy)
+            pairs = picked[:].bitcast(F32)
+            turned = psum.tile([P, 2, P], F32, name="turned%d" % c, tag="turned%d" % (c % 2))
+            for u in range(2):
+                nc.tensor.transpose(turned[:, u, :], pairs[:, u : SLOTS // 2 : 2], ident[:])
+            v_bf = held.tile([P, P * PACK], BF16, name="v_bf%d" % c, align_bytes=64)
+            nc.scalar.copy(
+                v_bf[:].bitcast(F32).rearrange("p (e u) -> p e u", u=2),
+                turned[:].rearrange("p u e -> p e u"),
+            )
+            nc.vector.quantize_mx(
+                out=v_codes[:, c * P : (c + 1) * P].bitcast(FP8X4),
+                scales=v_scales[:, c * P : (c + 1) * P],
+                in_=v_bf[:],
+            )
+
+        half_strict = held.tile([P, 1], F32, name="half_strict")
+        nc.gpsimd.tensor_scalar(half_strict[:], strict_col[:], 0.5, 0.0, ALU.mult, ALU.add)
+        sig = held.tile([P, PACK, P], F32, name="sig")
+        nc.vector.tensor_scalar(sig[:], th[:], half_strict[:], half_strict[:], ALU.mult, ALU.add)
+        neg_ts = held.tile([P, PACK, P], F32, name="neg_ts")
+        nc.vector.tensor_tensor(neg_ts[:], dealt(tb_bank[:]), sig[:], ALU.mult)
+
+        log_sig = held.tile([P, PACK, P], F32, name="log_sig")
+        soft = held.tile([P, PACK, P], F32, name="soft", align_bytes=64)
+        neg_s = held.tile([P, PACK, P], F32, name="neg_s", align_bytes=64)
+        for h in range(2):
+            nc.scalar.activation(half_of(log_sig, h), half_of(th_abs, h), ACT.Ln, scale=0.5, bias=0.5)
+        for h in range(2):
+            nc.vector.scalar_tensor_tensor(
+                half_of(soft, h), dealt(b_banks[h][:]), 0.0, half_of(log_sig, h), ALU.max, ALU.subtract
+            )
+        nc.vector.scalar_tensor_tensor(
+            neg_s[:], soft[:], strict_col[:], dealt(a_bank[:]), ALU.mult, ALU.subtract
+        )
+        neg_max = held.tile([P, 1], F32, name="neg_max")
+        nc.vector.tensor_reduce(neg_max[:], neg_s[:].rearrange("p r s -> p (r s)"), AX.X, ALU.min)
+        prob = held.tile([P, PACK, P], F32, name="prob")
+        z = held.tile([P, 1], F32, name="z")
+        nc.scalar.activation(prob[:], neg_s[:], ACT.Exp, scale=-1.0, bias=neg_max[:], accum_out=z[:])
+        rz = held.tile([P, 1], F32, name="rz")
+        nc.vector.reciprocal(rz[:], z[:])
+        neg_tp = held.tile([P, PACK, P], F32, name="neg_tp")
+        neg_tz = held.tile([P, 1], F32, name="neg_tz")
+        nc.vector.scalar_tensor_tensor(
+            neg_tp[:], neg_ts[:], rz[:], prob[:], ALU.mult, ALU.mult, accum_out=neg_tz[:]
+        )
+        coef = held.tile([P, 1], F32, name="coef")
+        nc.vector.tensor_scalar(coef[:], neg_tz[:], rz[:], None, ALU.mult)
+        tw = held.tile([P, PACK, P], F32, name="tw")
+        tw_turned = psum.tile([P, PACK, Q], F32, name="tw_turned")
+        for g in range(2):
+            rows = slice(2 * g, 2 * g + 2)
+            nc.vector.scalar_tensor_tensor(
+                tw[:, rows, :], prob[:, rows, :], coef[:], neg_tp[:, rows, :], ALU.mult, ALU.subtract
+            )
+            for r in range(2 * g, 2 * g + 2):
+                nc.tensor.transpose(tw_turned[:, r, :], tw[:, r, :], ident[:])
+        w_bf = held.tile([P, Q * PACK], BF16, name="w_bf", align_bytes=64)
+        nc.vector.tensor_tensor(
+            w_bf[:].rearrange("p (q r) -> p q r", r=PACK),
+            tw_turned[:].rearrange("p r q -> p q r"),
+            os_cols[:].unsqueeze(1).to_broadcast([P, Q, PACK]),
+            ALU.mult,
+        )
+        w_codes = held.tile([P, Q], U32, name="w_codes", align_bytes=64)
+        w_scales = held.tile([P, Q], U8, name="w_scales", align_bytes=64)
+        nc.vector.quantize_mx(out=w_codes[:].bitcast(FP8X4), scales=w_scales[:], in_=w_bf[:])
+
+        values(0, True, "picked0")
+        values(1, True, "picked1")
+        values(2, False, "neg_s")
+        values(3, False, "picked3")
+
+        for h in range(2):
+            cols = slice(h * (E // 2), (h + 1) * (E // 2))
+            bank = psum.tile([P, E // 2], F32, name="out_bank%d" % h, tag="half_bank%d" % h)
+            nc.tensor.matmul_mx(
+                out=bank[:],
+                lhsT=w_codes[:].bitcast(FP8X4),
+                lhsT_scale=w_scales[:],
+                rhs=v_codes[:, cols].bitcast(FP8X4),
+                rhs_scale=v_scales[:, cols],
+                start=True,
+                stop=True,
+            )
+            result = held.tile([P, E // 2], F32, name="result%d" % h)
+            if h == 0:
+                nc.vector.tensor_copy(result[:], bank[:])
+                nc.sync.dma_start(out[:, cols], result[:])
+            else:
+                nc.scalar.copy(result[:], bank[:])
+                nc.scalar.dma_start(out[:, cols], result[:])

@@ -19,6 +19,8 @@ P = 128
 PACK = 4
 D, E, T, SLOTS, Q = 512, 512, 2048, 512, 128
 HALF = SLOTS // 2
+LAST_SHARE = 192
+SHARE = 320
 FLOPS = 2 * Q * SLOTS * (3 * D + E)
 
 
@@ -27,183 +29,219 @@ def tile_attend_ttheldback_kernel(tc, query, query2, keys_words, keys_scales, st
     with ExitStack() as ctx:
         held = ctx.enter_context(tc.tile_pool(name="held", bufs=1))
         psum = ctx.enter_context(tc.psum_pool(name="psum", bufs=1))
+        halves = (slice(0, HALF), slice(HALF, SLOTS))
+
+        def load_query(name, source):
+            tile = held.tile([P, PACK, Q], F32, name=name, align_bytes=64)
+            nc.sync.dma_start(tile[:], source.rearrange("(p t) q -> p t q", t=PACK))
+            return tile
+
+        def load_values(c):
+            tile = held.tile([P, T], F32, name="val_pool%d" % c, align_bytes=64)
+            nc.sync.dma_start(tile[:], vals[c * P : (c + 1) * P, :])
+            return tile
+
+        def load_scales():
+            for quad in range(4):
+                nc.sync.dma_start(
+                    key_scale_pool[32 * quad : 32 * quad + 4, :].bitcast(I32),
+                    keys_scales[0, 4 * quad : 4 * quad + 4, :].bitcast(I32),
+                )
 
         key_scale_pool = held.tile([P, T], U8, name="key_scale_pool", align_bytes=64)
         nc.vector.memset(key_scale_pool[:].bitcast(I32), 0)
         offsets = held.tile([P, SLOTS // 16], U16, name="offsets")
         nc.sync.dma_start(offsets[:], offs)
-        for quad in range(4):
-            nc.scalar.dma_start(
-                key_scale_pool[32 * quad : 32 * quad + 4, :].bitcast(I32),
-                keys_scales[0, 4 * quad : 4 * quad + 4, :].bitcast(I32),
-            )
         key_word_pool = held.tile([P, T], U16, name="key_word_pool", align_bytes=64)
         nc.sync.dma_start(key_word_pool[:].bitcast(I32), keys_words[0].bitcast(I32))
-        raw = []
-        for name, source in (("b", query2), ("tb", dquery2), ("a", query)):
-            tile = held.tile([P, PACK, Q], F32, name="raw_" + name)
-            nc.sync.dma_start(tile[:], source.rearrange("(p t) q -> p t q", t=PACK))
-            raw.append(tile)
-        strict_col = held.tile([P, 1], F32, name="strict_col")
+        raw_b = load_query("raw_b", query2)
+        load_scales()
+        raw_a = load_query("raw_a", query)
+        raw_tb = load_query("raw_tb", dquery2)
+        val_pool = [load_values(c) for c in range(E // P)]
+        strict_col = held.tile([P, 1], F32, name="strict_col", align_bytes=64)
         nc.gpsimd.dma_start(strict_col[:], strict)
-        os_cols = held.tile([P, PACK], F32, name="os_cols")
-        nc.gpsimd.dma_start(os_cols[:], slot_factor.rearrange("o (p t) -> (o p) t", t=PACK))
-        val_pool = []
-        for c in range(E // P):
-            tile = held.tile([P, T], F32, name="val_pool%d" % c)
-            nc.sync.dma_start(tile[:], vals[c * P : (c + 1) * P, :])
-            val_pool.append(tile)
+        factor_cols = held.tile([P, PACK], F32, name="factor_cols")
+        nc.gpsimd.dma_start(factor_cols[:], slot_factor.rearrange("o (p t) -> (o p) t", t=PACK))
         ident = held.tile([P, P], F32, name="ident")
         make_identity(nc, ident[:])
+        slope = held.tile([P, 1], F32, name="slope")
+        nc.gpsimd.tensor_scalar(slope[:], strict_col[:], -0.5, 0.0, ALU.mult, ALU.add)
 
-        q_bf = held.tile([P, 3 * Q * PACK], BF16, name="q_bf", align_bytes=64)
-        q_codes = held.tile([P, 3 * Q], U32, name="q_codes", align_bytes=64)
-        q_scales = held.tile([P, 3 * Q], U8, name="q_scales", align_bytes=64)
+        def list_part(cols):
+            return offsets[:, cols.start // 16 : cols.stop // 16]
 
-        def round_query(j):
+        def quantize(name, rounded, tag):
+            width = rounded.shape[1] // PACK
+            codes = held.tile([P, width], U32, name=name + "_codes", tag=tag, align_bytes=64)
+            scales = held.tile([P, width], U8, name=name + "_scales", align_bytes=64)
+            nc.vector.quantize_mx(out=codes[:].bitcast(FP8X4), scales=scales[:], in_=rounded)
+            return codes, scales
+
+        def round_query(rounded, raw):
             nc.scalar.activation(
-                q_bf[:, j * Q * PACK : (j + 1) * Q * PACK].rearrange("p (q t) -> p q t", t=PACK),
-                raw[j][:].rearrange("p t q -> p q t"),
-                ACT.Copy,
-            )
-
-        def quantize_queries(j0, j1):
-            nc.vector.quantize_mx(
-                out=q_codes[:, j0 * Q : j1 * Q].bitcast(FP8X4),
-                scales=q_scales[:, j0 * Q : j1 * Q],
-                in_=q_bf[:, j0 * Q * PACK : j1 * Q * PACK],
+                rounded.rearrange("p (q t) -> p q t", t=PACK), raw[:].rearrange("p t q -> p q t"), ACT.Copy
             )
 
         key_words = held.tile([P, SLOTS], U16, name="key_words", align_bytes=64)
         key_scales = held.tile([P, SLOTS], U8, name="key_scales", align_bytes=64)
 
-        def gather_keys(h):
-            cols = slice(h * HALF, (h + 1) * HALF)
-            part = offsets[:, h * HALF // 16 : (h + 1) * HALF // 16]
-            nc.vector.tensor_copy(key_words[:, cols], key_word_pool[:].indirect(part))
-            nc.vector.tensor_copy(key_scales[:, cols], key_scale_pool[:].indirect(part))
-
-        def scores(bank, j, cols):
+        def scores(bank, rows, cols):
             nc.tensor.matmul_mx(
                 out=bank,
-                lhsT=q_codes[:, j * Q : (j + 1) * Q].bitcast(FP8X4),
-                lhsT_scale=q_scales[:, j * Q : (j + 1) * Q],
+                lhsT=rows[0].bitcast(FP8X4),
+                lhsT_scale=rows[1],
                 rhs=key_words[:, cols].bitcast(FP4X4),
                 rhs_scale=key_scales[:, cols],
                 start=True,
                 stop=True,
             )
 
-        def dealt(bank):
-            return bank.rearrange("p (s r) -> p r s", r=PACK)
-
-        def half_of(tile, h):
-            return tile[:, :, h * (P // 2) : (h + 1) * (P // 2)]
-
-        round_query(0)
-        gather_keys(0)
-        quantize_queries(0, 1)
-        gather_keys(1)
-        round_query(1)
-        round_query(2)
-        b_banks = [psum.tile([P, HALF], F32, name="half_bank%d" % h) for h in range(2)]
-        th = held.tile([P, PACK, P], F32, name="th")
-        th_abs = held.tile([P, PACK, P], F32, name="th_abs")
-        for h in range(2):
-            scores(b_banks[h][:], 0, slice(h * HALF, (h + 1) * HALF))
-            nc.scalar.activation(half_of(th, h), dealt(b_banks[h][:]), ACT.Tanh, scale=0.5)
-            nc.scalar.activation(half_of(th_abs, h), half_of(th, h), ACT.Abs)
-        quantize_queries(1, 3)
-        tb_bank = psum.tile([P, SLOTS], F32, name="tb_bank")
+        nc.vector.tensor_copy(key_words[:], key_word_pool[:].indirect(offsets[:]))
+        b_bf = held.tile([P, Q * PACK], BF16, name="b_bf", align_bytes=64)
+        round_query(b_bf[:], raw_b)
+        b_codes, b_scales = quantize("b", b_bf[:], "b_codes")
+        rows_b = (b_codes[:], b_scales[:])
+        for cols in halves:
+            nc.vector.tensor_copy(key_scales[:, cols], key_scale_pool[:].indirect(list_part(cols)))
+        rest_bf = held.tile([P, 2 * Q * PACK], BF16, name="rest_bf", align_bytes=64)
+        round_query(rest_bf[:, : Q * PACK], raw_a)
+        round_query(rest_bf[:, Q * PACK :], raw_tb)
+        rest_codes, rest_scales = quantize("rest", rest_bf[:], "key_scale_pool")
+        rows_a = (rest_codes[:, :Q], rest_scales[:, :Q])
+        rows_tb = (rest_codes[:, Q:], rest_scales[:, Q:])
+        b_banks = [psum.tile([P, HALF], F32, name="b_bank%d" % h) for h in range(2)]
+        th = held.tile([P, SLOTS], F32, name="th", tag="raw_tb", align_bytes=64)
+        for h, cols in enumerate(halves):
+            scores(b_banks[h][:], rows_b, cols)
+            nc.scalar.activation(th[:, cols], b_banks[h][:], ACT.Tanh, scale=0.5)
         a_bank = psum.tile([P, SLOTS], F32, name="a_bank")
-        scores(tb_bank[:], 1, slice(0, SLOTS))
-        scores(a_bank[:], 2, slice(0, SLOTS))
+        scores(a_bank[:], rows_a, slice(0, SLOTS))
 
         v_codes = held.tile([P, E], U32, name="v_codes", align_bytes=64)
         v_scales = held.tile([P, E], U8, name="v_scales", align_bytes=64)
 
-        def values(c, gather_on_vector, tag):
-            picked = held.tile([P, SLOTS], BF16, name="picked%d" % c, tag=tag, align_bytes=64)
-            if gather_on_vector:
-                nc.vector.tensor_copy(picked[:], val_pool[c][:].indirect(offsets[:]))
+        def gather_values(c, picked, cols, on_vector):
+            window = val_pool[c][:].indirect(list_part(cols))
+            if on_vector:
+                nc.vector.tensor_copy(picked[:, cols], window)
             else:
-                nc.scalar.activation(picked[:], val_pool[c][:].indirect(offsets[:]), ACT.Copy)
-            pairs = picked[:].bitcast(F32)
-            turned = psum.tile([P, 2, P], F32, name="turned%d" % c, tag="turned%d" % (c % 2))
-            for u in range(2):
-                nc.tensor.transpose(turned[:, u, :], pairs[:, u : SLOTS // 2 : 2], ident[:])
-            v_bf = held.tile([P, P * PACK], BF16, name="v_bf%d" % c, align_bytes=64)
-            nc.scalar.copy(
-                v_bf[:].bitcast(F32).rearrange("p (e u) -> p e u", u=2),
-                turned[:].rearrange("p u e -> p e u"),
-            )
-            nc.vector.quantize_mx(
-                out=v_codes[:, c * P : (c + 1) * P].bitcast(FP8X4),
-                scales=v_scales[:, c * P : (c + 1) * P],
-                in_=v_bf[:],
-            )
+                nc.scalar.activation(picked[:, cols], window, ACT.Copy)
 
-        half_strict = held.tile([P, 1], F32, name="half_strict")
-        nc.gpsimd.tensor_scalar(half_strict[:], strict_col[:], 0.5, 0.0, ALU.mult, ALU.add)
-        sig = held.tile([P, PACK, P], F32, name="sig")
-        nc.vector.tensor_scalar(sig[:], th[:], half_strict[:], half_strict[:], ALU.mult, ALU.add)
-        neg_ts = held.tile([P, PACK, P], F32, name="neg_ts")
-        nc.vector.tensor_tensor(neg_ts[:], dealt(tb_bank[:]), sig[:], ALU.mult)
+        def interleave(rounded, turned, on_vector):
+            words = rounded.bitcast(F32).rearrange("p (c e u) -> p c e u", e=P, u=2)
+            if on_vector:
+                nc.vector.tensor_copy(words, turned.rearrange("p c u e -> p c e u"))
+            else:
+                nc.scalar.copy(words, turned.rearrange("p c u e -> p c e u"))
 
-        log_sig = held.tile([P, PACK, P], F32, name="log_sig")
-        soft = held.tile([P, PACK, P], F32, name="soft", align_bytes=64)
-        neg_s = held.tile([P, PACK, P], F32, name="neg_s", align_bytes=64)
-        for h in range(2):
-            nc.scalar.activation(half_of(log_sig, h), half_of(th_abs, h), ACT.Ln, scale=0.5, bias=0.5)
-        for h in range(2):
+        def turn_values(first, chunks, on_vector, bank_tag, v_bf):
+            count = len(chunks)
+            turned = psum.tile([P, count, 2, P], F32, name="turned%d" % first, tag=bank_tag)
+            for c, chunk in enumerate(chunks):
+                pairs = chunk.bitcast(F32)
+                for u in range(2):
+                    nc.tensor.transpose(turned[:, c, u, :], pairs[:, u : SLOTS // 2 : 2], ident[:])
+            interleave(v_bf, turned[:], on_vector)
+            cols = slice(first * P, (first + count) * P)
+            nc.vector.quantize_mx(out=v_codes[:, cols].bitcast(FP8X4), scales=v_scales[:, cols], in_=v_bf)
+
+        whole = slice(0, SLOTS)
+        th_abs = held.tile([P, SLOTS], F32, name="th_abs")
+        for cols in halves:
+            nc.vector.scalar_tensor_tensor(th_abs[:, cols], th[:, cols], -1.0, th[:, cols], ALU.mult, ALU.max)
+        log_sig = held.tile([P, SLOTS], F32, name="log_sig")
+        for cols in halves:
+            nc.scalar.activation(log_sig[:, cols], th_abs[:, cols], ACT.Ln, scale=0.5, bias=0.5)
+        tb_bank = psum.tile([P, SLOTS], F32, name="tb_bank")
+        scores(tb_bank[:], rows_tb, whole)
+        sig = held.tile([P, SLOTS], F32, name="sig")
+        nc.vector.tensor_scalar(sig[:], th[:], slope[:], slope[:], ALU.mult, ALU.add)
+        ts = held.tile([P, SLOTS], F32, name="ts")
+        nc.vector.tensor_tensor(ts[:], tb_bank[:], sig[:], ALU.mult)
+        picked0 = held.tile([P, SLOTS], BF16, name="picked0", align_bytes=64)
+        gather_values(0, picked0[:], whole, True)
+
+        work = held.tile([P, 2 * SLOTS], F32, name="work", tag="val_pool0", align_bytes=64)
+        soft = work[:, :SLOTS]
+        neg_s = work[:, SLOTS:]
+        for h, cols in enumerate(halves):
             nc.vector.scalar_tensor_tensor(
-                half_of(soft, h), dealt(b_banks[h][:]), 0.0, half_of(log_sig, h), ALU.max, ALU.subtract
+                soft[:, cols], b_banks[h][:], 0.0, log_sig[:, cols], ALU.max, ALU.subtract
             )
-        nc.vector.scalar_tensor_tensor(
-            neg_s[:], soft[:], strict_col[:], dealt(a_bank[:]), ALU.mult, ALU.subtract
-        )
-        neg_max = held.tile([P, 1], F32, name="neg_max")
-        nc.vector.tensor_reduce(neg_max[:], neg_s[:].rearrange("p r s -> p (r s)"), AX.X, ALU.min)
-        prob = held.tile([P, PACK, P], F32, name="prob")
+        for cols in halves:
+            nc.vector.scalar_tensor_tensor(
+                neg_s[:, cols], soft[:, cols], strict_col[:], a_bank[:, cols], ALU.mult, ALU.subtract
+            )
+        neg_max = held.tile([P, 1], F32, name="neg_max", align_bytes=64)
+        nc.vector.tensor_reduce(neg_max[:], neg_s, AX.X, ALU.min)
+        prob = held.tile([P, SLOTS], F32, name="prob")
         z = held.tile([P, 1], F32, name="z")
-        nc.scalar.activation(prob[:], neg_s[:], ACT.Exp, scale=-1.0, bias=neg_max[:], accum_out=z[:])
+        nc.scalar.activation(prob[:], neg_s, ACT.Exp, scale=-1.0, bias=neg_max[:], accum_out=z[:])
+
+        v_bf0 = held.tile([P, P * PACK], BF16, name="v_bf0", tag="strict_col", align_bytes=64)
+        turn_values(0, [picked0[:]], True, "turned0", v_bf0[:])
+        factor_bank = psum.tile([P, PACK, P], F32, name="factor_bank", tag="b_bank0")
+        for r in range(PACK):
+            nc.tensor.transpose(factor_bank[:, r, :], factor_cols[:, r : r + 1].to_broadcast([P, P]), ident[:])
+        picked1 = work[:, SLOTS - SHARE // 2 : SLOTS + (SLOTS - SHARE) // 2].bitcast(BF16)
+        gather_values(1, picked1, slice(0, SHARE), True)
+
         rz = held.tile([P, 1], F32, name="rz")
         nc.vector.reciprocal(rz[:], z[:])
-        neg_tp = held.tile([P, PACK, P], F32, name="neg_tp")
-        neg_tz = held.tile([P, 1], F32, name="neg_tz")
-        nc.vector.scalar_tensor_tensor(
-            neg_tp[:], neg_ts[:], rz[:], prob[:], ALU.mult, ALU.mult, accum_out=neg_tz[:]
-        )
-        coef = held.tile([P, 1], F32, name="coef")
-        nc.vector.tensor_scalar(coef[:], neg_tz[:], rz[:], None, ALU.mult)
-        tw = held.tile([P, PACK, P], F32, name="tw")
-        tw_turned = psum.tile([P, PACK, Q], F32, name="tw_turned")
-        for g in range(2):
-            rows = slice(2 * g, 2 * g + 2)
+        tp = held.tile([P, SLOTS], F32, name="tp")
+        tz = held.tile([P, 1], F32, name="tz")
+        nc.vector.scalar_tensor_tensor(tp[:], ts[:], 1.0, prob[:], ALU.mult, ALU.mult, accum_out=tz[:])
+        late_work = held.tile([P, SLOTS + HALF], F32, name="late_work", align_bytes=64)
+        weight = [late_work[:, cols] for cols in halves]
+
+        def pair(tile, u):
+            return tile.rearrange("p (s r) -> p s r", r=PACK)[:, :, 2 * u : 2 * u + 2]
+
+        def weigh(u):
             nc.vector.scalar_tensor_tensor(
-                tw[:, rows, :], prob[:, rows, :], coef[:], neg_tp[:, rows, :], ALU.mult, ALU.subtract
+                weight[u].rearrange("p (s e) -> p s e", e=2),
+                pair(prob[:], u),
+                rz[:],
+                factor_bank[:, 2 * u : 2 * u + 2, :].rearrange("p e s -> p s e"),
+                ALU.mult,
+                ALU.mult,
             )
-            for r in range(2 * g, 2 * g + 2):
-                nc.tensor.transpose(tw_turned[:, r, :], tw[:, r, :], ident[:])
-        w_bf = held.tile([P, Q * PACK], BF16, name="w_bf", align_bytes=64)
-        nc.vector.tensor_tensor(
-            w_bf[:].rearrange("p (q r) -> p q r", r=PACK),
-            tw_turned[:].rearrange("p r q -> p q r"),
-            os_cols[:].unsqueeze(1).to_broadcast([P, Q, PACK]),
-            ALU.mult,
-        )
-        w_codes = held.tile([P, Q], U32, name="w_codes", align_bytes=64)
-        w_scales = held.tile([P, Q], U8, name="w_scales", align_bytes=64)
-        nc.vector.quantize_mx(out=w_codes[:].bitcast(FP8X4), scales=w_scales[:], in_=w_bf[:])
 
-        values(0, True, "picked0")
-        values(1, True, "picked1")
-        values(2, False, "neg_s")
-        values(3, False, "picked3")
+        weigh(0)
+        mean_ts = held.tile([P, 1], F32, name="mean_ts")
+        nc.vector.tensor_scalar(mean_ts[:], tz[:], rz[:], None, ALU.mult)
+        weigh(1)
+        w_pairs = held.tile([P, 2, HALF], BF16, name="w_pairs")
+        w_turned = psum.tile([P, 1, 2, Q], F32, name="w_turned", tag="b_bank1")
+        for u in range(2):
+            nc.vector.scalar_tensor_tensor(
+                w_pairs[:, u, :].rearrange("p (s e) -> p s e", e=2),
+                pair(ts[:], u),
+                mean_ts[:],
+                weight[u].rearrange("p (s e) -> p s e", e=2),
+                ALU.subtract,
+                ALU.mult,
+            )
+            nc.tensor.transpose(w_turned[:, 0, u, :], w_pairs[:, u, :].bitcast(F32), ident[:])
 
-        for h in range(2):
-            cols = slice(h * (E // 2), (h + 1) * (E // 2))
-            bank = psum.tile([P, E // 2], F32, name="out_bank%d" % h, tag="half_bank%d" % h)
+        gather_values(1, picked1, slice(SHARE, SLOTS), False)
+        picked2 = held.tile([P, SLOTS], BF16, name="picked2", tag="neg_max", align_bytes=64)
+        gather_values(2, picked2[:], whole, False)
+        picked3 = late_work[:, SLOTS - LAST_SHARE // 2 : SLOTS + (SLOTS - LAST_SHARE) // 2].bitcast(BF16)
+        gather_values(3, picked3, slice(0, LAST_SHARE), True)
+        gather_values(3, picked3, slice(LAST_SHARE, SLOTS), False)
+        late_bf = held.tile([P, 3 * P * PACK], BF16, name="late_bf", tag="val_pool3", align_bytes=64)
+        w_bf = late_bf[:, : Q * PACK]
+        interleave(w_bf, w_turned[:], False)
+        w_codes, w_scales = quantize("w", w_bf, "w_codes")
+        turn_values(1, [picked1, picked2[:]], True, "turned1", late_bf[:, Q * PACK :])
+        v_bf3 = held.tile([P, P * PACK], BF16, name="v_bf3", align_bytes=64)
+        turn_values(3, [picked3], False, "turned3", v_bf3[:])
+
+        for start, stop, tag, result_tag, on_vector in ((0, 256, "turned0", "late_work", False), (256, 384, "turned1", "v_bf3", True), (384, 512, "a_bank", "result384", True)):
+            cols = slice(start, stop)
+            bank = psum.tile([P, stop - start], F32, name="out_bank%d" % start, tag=tag)
             nc.tensor.matmul_mx(
                 out=bank[:],
                 lhsT=w_codes[:].bitcast(FP8X4),
@@ -213,10 +251,9 @@ def tile_attend_ttheldback_kernel(tc, query, query2, keys_words, keys_scales, st
                 start=True,
                 stop=True,
             )
-            result = held.tile([P, E // 2], F32, name="result%d" % h)
-            if h == 0:
+            result = held.tile([P, stop - start], F32, name="result%d" % start, tag=result_tag, align_bytes=64)
+            if on_vector:
                 nc.vector.tensor_copy(result[:], bank[:])
-                nc.sync.dma_start(out[:, cols], result[:])
             else:
                 nc.scalar.copy(result[:], bank[:])
-                nc.scalar.dma_start(out[:, cols], result[:])
+            nc.sync.dma_start(out[:, cols], result[:])

from contextlib import ExitStack

import concourse.mybir as mybir
from concourse.masks import make_identity

F32 = mybir.dt.float32
BF16 = mybir.dt.bfloat16
I32 = mybir.dt.int32
U32 = mybir.dt.uint32
U16 = mybir.dt.uint16
U8 = mybir.dt.uint8
FP8X4 = mybir.dt.float8_e4m3fn_x4
FP4X4 = mybir.dt.float4_e2m1fn_x4
ALU = mybir.AluOpType
ACT = mybir.ActivationFunctionType
AX = mybir.AxisListType

P = 128
PACK = 4
D, E, T, SLOTS, Q = 512, 512, 2048, 512, 128
HALF = SLOTS // 2
LAST_SHARE = 192
SHARE = 320
FLOPS = 2 * Q * SLOTS * (3 * D + E)


def tile_attend_ttheldback_kernel(tc, query, query2, keys_words, keys_scales, strict, dquery2, slot_factor, vals, offs, out):
    nc = tc.nc
    with ExitStack() as ctx:
        held = ctx.enter_context(tc.tile_pool(name="held", bufs=1))
        psum = ctx.enter_context(tc.psum_pool(name="psum", bufs=1))
        halves = (slice(0, HALF), slice(HALF, SLOTS))

        def load_query(name, source):
            tile = held.tile([P, PACK, Q], F32, name=name, align_bytes=64)
            nc.sync.dma_start(tile[:], source.rearrange("(p t) q -> p t q", t=PACK))
            return tile

        def load_values(c):
            tile = held.tile([P, T], F32, name="val_pool%d" % c, align_bytes=64)
            nc.sync.dma_start(tile[:], vals[c * P : (c + 1) * P, :])
            return tile

        def load_scales():
            for quad in range(4):
                nc.sync.dma_start(
                    key_scale_pool[32 * quad : 32 * quad + 4, :].bitcast(I32),
                    keys_scales[0, 4 * quad : 4 * quad + 4, :].bitcast(I32),
                )

        key_scale_pool = held.tile([P, T], U8, name="key_scale_pool", align_bytes=64)
        nc.vector.memset(key_scale_pool[:].bitcast(I32), 0)
        offsets = held.tile([P, SLOTS // 16], U16, name="offsets")
        nc.sync.dma_start(offsets[:], offs)
        key_word_pool = held.tile([P, T], U16, name="key_word_pool", align_bytes=64)
        nc.sync.dma_start(key_word_pool[:].bitcast(I32), keys_words[0].bitcast(I32))
        raw_b = load_query("raw_b", query2)
        load_scales()
        raw_a = load_query("raw_a", query)
        raw_tb = load_query("raw_tb", dquery2)
        val_pool = [load_values(c) for c in range(E // P)]
        strict_col = held.tile([P, 1], F32, name="strict_col", align_bytes=64)
        nc.gpsimd.dma_start(strict_col[:], strict)
        factor_cols = held.tile([P, PACK], F32, name="factor_cols")
        nc.gpsimd.dma_start(factor_cols[:], slot_factor.rearrange("o (p t) -> (o p) t", t=PACK))
        ident = held.tile([P, P], F32, name="ident")
        make_identity(nc, ident[:])
        slope = held.tile([P, 1], F32, name="slope")
        nc.gpsimd.tensor_scalar(slope[:], strict_col[:], -0.5, 0.0, ALU.mult, ALU.add)

        def list_part(cols):
            return offsets[:, cols.start // 16 : cols.stop // 16]

        def quantize(name, rounded, tag):
            width = rounded.shape[1] // PACK
            codes = held.tile([P, width], U32, name=name + "_codes", tag=tag, align_bytes=64)
            scales = held.tile([P, width], U8, name=name + "_scales", align_bytes=64)
            nc.vector.quantize_mx(out=codes[:].bitcast(FP8X4), scales=scales[:], in_=rounded)
            return codes, scales

        def round_query(rounded, raw):
            nc.scalar.activation(
                rounded.rearrange("p (q t) -> p q t", t=PACK), raw[:].rearrange("p t q -> p q t"), ACT.Copy
            )

        key_words = held.tile([P, SLOTS], U16, name="key_words", align_bytes=64)
        key_scales = held.tile([P, SLOTS], U8, name="key_scales", align_bytes=64)

        def scores(bank, rows, cols):
            nc.tensor.matmul_mx(
                out=bank,
                lhsT=rows[0].bitcast(FP8X4),
                lhsT_scale=rows[1],
                rhs=key_words[:, cols].bitcast(FP4X4),
                rhs_scale=key_scales[:, cols],
                start=True,
                stop=True,
            )

        nc.vector.tensor_copy(key_words[:], key_word_pool[:].indirect(offsets[:]))
        b_bf = held.tile([P, Q * PACK], BF16, name="b_bf", align_bytes=64)
        round_query(b_bf[:], raw_b)
        b_codes, b_scales = quantize("b", b_bf[:], "b_codes")
        rows_b = (b_codes[:], b_scales[:])
        for cols in halves:
            nc.vector.tensor_copy(key_scales[:, cols], key_scale_pool[:].indirect(list_part(cols)))
        rest_bf = held.tile([P, 2 * Q * PACK], BF16, name="rest_bf", align_bytes=64)
        round_query(rest_bf[:, : Q * PACK], raw_a)
        round_query(rest_bf[:, Q * PACK :], raw_tb)
        rest_codes, rest_scales = quantize("rest", rest_bf[:], "key_scale_pool")
        rows_a = (rest_codes[:, :Q], rest_scales[:, :Q])
        rows_tb = (rest_codes[:, Q:], rest_scales[:, Q:])
        b_banks = [psum.tile([P, HALF], F32, name="b_bank%d" % h) for h in range(2)]
        th = held.tile([P, SLOTS], F32, name="th", tag="raw_tb", align_bytes=64)
        for h, cols in enumerate(halves):
            scores(b_banks[h][:], rows_b, cols)
            nc.scalar.activation(th[:, cols], b_banks[h][:], ACT.Tanh, scale=0.5)
        a_bank = psum.tile([P, SLOTS], F32, name="a_bank")
        scores(a_bank[:], rows_a, slice(0, SLOTS))

        v_codes = held.tile([P, E], U32, name="v_codes", align_bytes=64)
        v_scales = held.tile([P, E], U8, name="v_scales", align_bytes=64)

        def gather_values(c, picked, cols, on_vector):
            window = val_pool[c][:].indirect(list_part(cols))
            if on_vector:
                nc.vector.tensor_copy(picked[:, cols], window)
            else:
                nc.scalar.activation(picked[:, cols], window, ACT.Copy)

        def interleave(rounded, turned, on_vector):
            words = rounded.bitcast(F32).rearrange("p (c e u) -> p c e u", e=P, u=2)
            if on_vector:
                nc.vector.tensor_copy(words, turned.rearrange("p c u e -> p c e u"))
            else:
                nc.scalar.copy(words, turned.rearrange("p c u e -> p c e u"))

        def turn_values(first, chunks, on_vector, bank_tag, v_bf):
            count = len(chunks)
            turned = psum.tile([P, count, 2, P], F32, name="turned%d" % first, tag=bank_tag)
            for c, chunk in enumerate(chunks):
                pairs = chunk.bitcast(F32)
                for u in range(2):
                    nc.tensor.transpose(turned[:, c, u, :], pairs[:, u : SLOTS // 2 : 2], ident[:])
            interleave(v_bf, turned[:], on_vector)
            cols = slice(first * P, (first + count) * P)
            nc.vector.quantize_mx(out=v_codes[:, cols].bitcast(FP8X4), scales=v_scales[:, cols], in_=v_bf)

        whole = slice(0, SLOTS)
        th_abs = held.tile([P, SLOTS], F32, name="th_abs")
        for cols in halves:
            nc.vector.scalar_tensor_tensor(th_abs[:, cols], th[:, cols], -1.0, th[:, cols], ALU.mult, ALU.max)
        log_sig = held.tile([P, SLOTS], F32, name="log_sig")
        for cols in halves:
            nc.scalar.activation(log_sig[:, cols], th_abs[:, cols], ACT.Ln, scale=0.5, bias=0.5)
        tb_bank = psum.tile([P, SLOTS], F32, name="tb_bank")
        scores(tb_bank[:], rows_tb, whole)
        sig = held.tile([P, SLOTS], F32, name="sig")
        nc.vector.tensor_scalar(sig[:], th[:], slope[:], slope[:], ALU.mult, ALU.add)
        ts = held.tile([P, SLOTS], F32, name="ts")
        nc.vector.tensor_tensor(ts[:], tb_bank[:], sig[:], ALU.mult)
        picked0 = held.tile([P, SLOTS], BF16, name="picked0", align_bytes=64)
        gather_values(0, picked0[:], whole, True)

        work = held.tile([P, 2 * SLOTS], F32, name="work", tag="val_pool0", align_bytes=64)
        soft = work[:, :SLOTS]
        neg_s = work[:, SLOTS:]
        for h, cols in enumerate(halves):
            nc.vector.scalar_tensor_tensor(
                soft[:, cols], b_banks[h][:], 0.0, log_sig[:, cols], ALU.max, ALU.subtract
            )
        for cols in halves:
            nc.vector.scalar_tensor_tensor(
                neg_s[:, cols], soft[:, cols], strict_col[:], a_bank[:, cols], ALU.mult, ALU.subtract
            )
        neg_max = held.tile([P, 1], F32, name="neg_max", align_bytes=64)
        nc.vector.tensor_reduce(neg_max[:], neg_s, AX.X, ALU.min)
        prob = held.tile([P, SLOTS], F32, name="prob")
        z = held.tile([P, 1], F32, name="z")
        nc.scalar.activation(prob[:], neg_s, ACT.Exp, scale=-1.0, bias=neg_max[:], accum_out=z[:])

        v_bf0 = held.tile([P, P * PACK], BF16, name="v_bf0", tag="strict_col", align_bytes=64)
        turn_values(0, [picked0[:]], True, "turned0", v_bf0[:])
        factor_bank = psum.tile([P, PACK, P], F32, name="factor_bank", tag="b_bank0")
        for r in range(PACK):
            nc.tensor.transpose(factor_bank[:, r, :], factor_cols[:, r : r + 1].to_broadcast([P, P]), ident[:])
        picked1 = work[:, SLOTS - SHARE // 2 : SLOTS + (SLOTS - SHARE) // 2].bitcast(BF16)
        gather_values(1, picked1, slice(0, SHARE), True)

        rz = held.tile([P, 1], F32, name="rz")
        nc.vector.reciprocal(rz[:], z[:])
        tp = held.tile([P, SLOTS], F32, name="tp")
        tz = held.tile([P, 1], F32, name="tz")
        nc.vector.scalar_tensor_tensor(tp[:], ts[:], 1.0, prob[:], ALU.mult, ALU.mult, accum_out=tz[:])
        late_work = held.tile([P, SLOTS + HALF], F32, name="late_work", align_bytes=64)
        weight = [late_work[:, cols] for cols in halves]

        def pair(tile, u):
            return tile.rearrange("p (s r) -> p s r", r=PACK)[:, :, 2 * u : 2 * u + 2]

        def weigh(u):
            nc.vector.scalar_tensor_tensor(
                weight[u].rearrange("p (s e) -> p s e", e=2),
                pair(prob[:], u),
                rz[:],
                factor_bank[:, 2 * u : 2 * u + 2, :].rearrange("p e s -> p s e"),
                ALU.mult,
                ALU.mult,
            )

        weigh(0)
        mean_ts = held.tile([P, 1], F32, name="mean_ts")
        nc.vector.tensor_scalar(mean_ts[:], tz[:], rz[:], None, ALU.mult)
        weigh(1)
        w_pairs = held.tile([P, 2, HALF], BF16, name="w_pairs")
        w_turned = psum.tile([P, 1, 2, Q], F32, name="w_turned", tag="b_bank1")
        for u in range(2):
            nc.vector.scalar_tensor_tensor(
                w_pairs[:, u, :].rearrange("p (s e) -> p s e", e=2),
                pair(ts[:], u),
                mean_ts[:],
                weight[u].rearrange("p (s e) -> p s e", e=2),
                ALU.subtract,
                ALU.mult,
            )
            nc.tensor.transpose(w_turned[:, 0, u, :], w_pairs[:, u, :].bitcast(F32), ident[:])

        gather_values(1, picked1, slice(SHARE, SLOTS), False)
        picked2 = held.tile([P, SLOTS], BF16, name="picked2", tag="neg_max", align_bytes=64)
        gather_values(2, picked2[:], whole, False)
        picked3 = late_work[:, SLOTS - LAST_SHARE // 2 : SLOTS + (SLOTS - LAST_SHARE) // 2].bitcast(BF16)
        gather_values(3, picked3, slice(0, LAST_SHARE), True)
        gather_values(3, picked3, slice(LAST_SHARE, SLOTS), False)
        late_bf = held.tile([P, 3 * P * PACK], BF16, name="late_bf", tag="val_pool3", align_bytes=64)
        w_bf = late_bf[:, : Q * PACK]
        interleave(w_bf, w_turned[:], False)
        w_codes, w_scales = quantize("w", w_bf, "w_codes")
        turn_values(1, [picked1, picked2[:]], True, "turned1", late_bf[:, Q * PACK :])
        v_bf3 = held.tile([P, P * PACK], BF16, name="v_bf3", align_bytes=64)
        turn_values(3, [picked3], False, "turned3", v_bf3[:])

        for start, stop, tag, result_tag, on_vector in ((0, 256, "turned0", "late_work", False), (256, 384, "turned1", "v_bf3", True), (384, 512, "a_bank", "result384", True)):
            cols = slice(start, stop)
            bank = psum.tile([P, stop - start], F32, name="out_bank%d" % start, tag=tag)
            nc.tensor.matmul_mx(
                out=bank[:],
                lhsT=w_codes[:].bitcast(FP8X4),
                lhsT_scale=w_scales[:],
                rhs=v_codes[:, cols].bitcast(FP8X4),
                rhs_scale=v_scales[:, cols],
                start=True,
                stop=True,
            )
            result = held.tile([P, stop - start], F32, name="result%d" % start, tag=result_tag, align_bytes=64)
            if on_vector:
                nc.vector.tensor_copy(result[:], bank[:])
            else:
                nc.scalar.copy(result[:], bank[:])
            nc.sync.dma_start(out[:, cols], result[:])
